import numpy as np, ml_dtypes
CORES = [24,32,56,88,96,104,30,38,62,94,102,110]
N = 12
KB, QP = 1, 32
MEM = [4,10]
def setup_inputs(rng):
    q = rng.standard_normal((N, 128, QP), dtype=np.float32) / 4; k = rng.standard_normal((N, 128, KB * 128), dtype=np.float32)
    a = 2 * np.pi * rng.random((N, QP)); s = 400 * rng.random((N, QP)) ** 1.5; q[:, 0, :] = s * np.cos(a); q[:, 1, :] = s * np.sin(a); q[:, 2, :] = 150 * rng.standard_normal((N, QP)); k[:, 2, :] = 1 + k[:, 2, :] / 50
    c = np.zeros(N); c[MEM] = rng.permutation(len(MEM))
    a = (2 * np.pi * rng.random() + np.pi / 2 * (c.reshape(N, 1, 1) + 0.5) / len(MEM) - 0.5 + (np.arange(KB).reshape(1, KB, 1) + rng.random((N, KB, 128))) / KB).reshape(N, KB * 128); k[:, 0, :] = np.cos(a); k[:, 1, :] = np.sin(a)
    return {"q": q.astype(ml_dtypes.bfloat16), "k": k.astype(ml_dtypes.bfloat16), "v": rng.standard_normal((N, 128, KB * 128), dtype=np.float32).astype(ml_dtypes.bfloat16)}
def setup_inputs_big(rng):
    d = setup_inputs(rng)
    for k in ("v",): d[k] = (d[k].astype(np.float32) * 1048576.0).astype(d[k].dtype)
    return d
def setup_inputs_small(rng):
    d = setup_inputs(rng)
    for k in ("v",): d[k] = (d[k].astype(np.float32) * (1 / 1048576.0)).astype(d[k].dtype)
    return d
def reference(q, k, v):
    Q, K, V = q.astype(np.float64), k.astype(np.float64), v.astype(np.float64)
    y = np.zeros((N, QP, 128))
    for r in range(N):
        js = list(MEM)
        S = np.concatenate([K[j].T @ Q[r] for j in js], axis=0)
        P = np.exp(S - S.max(axis=0)); P = P / P.sum(axis=0)
        y[r] = P.T @ np.concatenate([V[j][:, 128 * b:128 * b + 128] for j in js for b in range(KB)], axis=0)
    return {"y": y.astype(ml_dtypes.bfloat16)}

@@ -1,0 +1,249 @@
+from concourse.bass import DstId, RemoteDMATransfer
+from concourse.mybir import AluOpType, AxisListType, ActivationFunctionType
+
+NQ = 8
+NR = 2
+MAXP = 3
+BF, F32 = "bfloat16", "float32"
+
+SCRATCH = {
+    "qd": ("dram", [128, 32], BF),
+    "qr": ("dram", [2, 128, 32], BF),
+    "yl": ("sbuf", [128, 32], BF),
+    "kv": ("sbuf", [128, 512], BF),
+    "ql": ("sbuf", [128, 32 * 4 * MAXP], BF),
+    "ones": ("sbuf", [128, 128], BF),
+    "ident": ("sbuf", [128, 128], BF),
+    "ee": ("sbuf", [128, 128], BF),
+    "rep": ("sbuf", [128, 128], BF),
+    "mask": ("sbuf", [128, 4], F32),
+    "nm": ("sbuf", [128, 4], F32),
+    "ls": ("sbuf", [128, 4], F32),
+    "rs": ("sbuf", [128, 4], F32),
+    "rm": ("sbuf", [128, 4 * MAXP], BF),
+    "pp": ("sbuf", [128, 256 * MAXP], BF),
+    "pt": ("sbuf", [128, 256 * MAXP], BF),
+    "ys": ("sbuf", [128, 128 * MAXP], BF),
+    "pa": ("psum", [128, 512], F32),
+    "pr": ("psum", [128, 512], F32),
+    "y0": ("psum", [128, 512], F32),
+    "y1": ("psum", [128, 512], F32),
+    "y2": ("psum", [128, 512], F32),
+    "y3": ("psum", [128, 512], F32),
+}
+SEMAPHORES = ["ld", "rel0", "rel1", "sent", "yarr", "st", "kvld", "kva", "qa0", "qa1", "qa2",
+              "sA", "sB", "sD", "sF", "sK", "sS", "sM", "sE", "sT", "sC", "sR1", "sR2", "sRR",
+              "sY0", "sY1", "sY2", "sY3", "sO"]
+
+
+def _bits(mask):
+    return [i for i in range(16) if (mask >> i) & 1]
+
+
+def _pick(bits, n):
+    step = len(bits) // n
+    m = 0
+    for b in bits[::step][:n]:
+        m |= 1 << b
+    return m
+
+
+def _plan(T, topo):
+    cores = list(T.cores)
+    mem = [cores[j] for j in T.tables["MEM"]]
+    clients = [c for c in cores if c not in mem]
+    opts = {c: [s for s in mem if topo.may_write(s, c)] for c in clients}
+    load = {s: 1 for s in mem}
+    server = {}
+    for c in sorted(clients, key=lambda c: len(opts[c])):
+        s = min(opts[c], key=lambda x: load[x])
+        server[c] = s
+        load[s] += 1
+    via = {}
+    for c in clients:
+        s = server[c]
+        if topo.may_write(c, s):
+            via[c] = None
+        else:
+            via[c] = [x for x in clients if x != c and topo.chip(x) == topo.chip(c) and server[x] == s
+                      and topo.may_write(x, s)][0]
+    passes = {}
+    for s in mem:
+        ps = [[s]]
+        for grp in ([c for c in clients if server[c] == s and via[c] is None],
+                    [c for c in clients if server[c] == s and via[c] is not None]):
+            for i in range(0, len(grp), 4):
+                ps.append(grp[i:i + 4])
+        passes[s] = ps
+    place = {}
+    for s in mem:
+        col = 0
+        for i, blk in enumerate(ps_ for ps_ in passes[s]):
+            for c in blk:
+                w = 0
+                if c != s:
+                    eng = _bits(topo.mask(s, c))
+                    w = 1
+                    while w * 2 * len(blk) <= len(eng):
+                        w *= 2
+                place[c] = (i, col, w)
+                col += 32
+    return mem, server, via, passes, place
+
+
+def _store_y(queues, T, src, sem_wait, val):
+    for q in queues:
+        q.wait_ge(sem_wait, val)
+    for fb in range(4):
+        q = queues[fb % len(queues)]
+        q.dma_start(T.y[:, 32 * fb:32 * fb + 32], src[32 * fb:32 * fb + 32, :]).then_inc(T.sem.st, 16)
+
+
+def _client(g, core, T, topo, plan):
+    mem, server, via, passes, place = plan
+    s = server[core]
+    rid, pid, _ = topo.addr(s)
+    g.sync.dma_start(T.qd[:, :], T.q[:, :]).then_inc(T.sem.ld, 16)
+    g.wait_ge(T.sem.ld, 16)
+    sent = 0
+    if via[core] is None:
+        i, col, _w = place[core]
+        m = _pick(_bits(topo.mask(core, s)), NQ)
+        g.remote_dma(T.ql[:, col:col + 32], T.qd[:, :], T.sem["qa%d" % i], T.sem.sent, pid, rid, m)
+        sent += NQ
+        for k, c in enumerate([c for c in via if via[c] == core]):
+            i, col, _w = place[c]
+            g.wait_ge(T.sem["rel%d" % k], NR)
+            g.remote_dma(T.ql[:, col:col + 32], T.qr[k], T.sem["qa%d" % i], T.sem.sent, pid, rid, m)
+            sent += NQ
+    else:
+        x = via[core]
+        k = [c for c in via if via[c] == x].index(core)
+        xr, xp, _ = topo.addr(x)
+        g.remote_dma(T.qr[k], T.qd[:, :], T.sem["rel%d" % k], T.sem.sent, xp, xr,
+                     _pick(_bits(topo.mask(core, x)), NR))
+        sent += NR
+    _store_y([g.sync, g.scalar], T, T.yl, T.sem.yarr, place[core][2])
+    g.wait_ge(T.sem.sent, sent)
+    g.wait_ge(T.sem.st, 64)
+
+
+def _server(g, core, T, topo, plan):
+    mem, server, via, passes, place = plan
+    S = T.sem
+    pe, dve, act = g.tensor, g.vector, g.scalar
+    me = mem.index(core)
+    n = {}
+
+    def inc(instr, name, k=1):
+        instr.then_inc(S[name], k)
+        n[name] = n.get(name, 0) + k
+
+    o = 256 * me
+    g.sync.dma_start(T.kv[:, o:o + 128], T.k[:, :]).then_inc(S.kvld, 16)
+    act.dma_start(T.kv[:, o + 128:o + 256], T.v[:, :]).then_inc(S.kvld, 16)
+    g.sync.dma_start(T.ql[:, 0:32], T.q[:, :]).then_inc(S.qa0, 16)
+
+    inc(dve.memset(T.ones[:, :], 1.0), "sA")
+    inc(dve.memset(T.mask[:, :], 0.0), "sK")
+    dve.wait_ge(S.sK, 1)
+    for b in range(4):
+        inc(dve.memset(T.mask[32 * b:32 * b + 32, b:b + 1], 1.0), "sK")
+    dve.wait_ge(S.sK, 5)
+    g.wait_ge(S.sA, 1)
+    inc(g.affine_select(T.ident[:, :], T.ones[:, :], [[-1, 128]], AluOpType.is_equal, 0.0, 0, 1), "sB")
+    inc(g.affine_select(T.ee[0:32, :], T.ones[0:32, :], [[0, 4], [-1, 32]], AluOpType.is_equal, 0.0, 0, 1), "sB")
+    pe.wait_ge(S.sB, 2)
+    inc(pe.matmul(T.pr[:, 0:128], T.ee[0:32, :], T.ee[0:32, :], True, True), "sD")
+    dve.wait_ge(S.sD, 1)
+    inc(dve.tensor_copy(T.rep[:, :], T.pr[:, 0:128]), "sF")
+    pe.wait_ge(S.sF, 1)
+
+    dsts = [c for ps in passes[core] for c in ps if c != core] + [x for x in mem if x != core]
+    common = 0xFFFF
+    for d in dsts:
+        common &= topo.mask(core, d)
+    eng = _bits(common)
+    sent = 0
+    g.wait_ge(S.kvld, 32)
+    for x in mem:
+        if x != core:
+            xr, xp, _ = topo.addr(x)
+            g.remote_dma(T.kv[:, o:o + 256], T.kv[:, o:o + 256], S.kva, S.sent, xp, xr, _pick(eng, len(eng)))
+            sent += len(eng)
+    pe.wait_ge(S.kvld, 32)
+    pe.wait_ge(S.kva, len(eng) * (len(mem) - 1))
+
+    ybank = [T.y0, T.y1, T.y2, T.y3]
+    col = 0
+    for p, blk in enumerate(passes[core]):
+        nb = len(blk)
+        Q = 32 * nb
+        P0 = 256 * p
+        pe.wait_ge(S["qa%d" % p], 16 if p == 0 else NQ * nb)
+        for kb in range(2):
+            inc(pe.matmul(T.pa[0:Q, 128 * kb:128 * kb + 128], T.ql[:, col:col + Q],
+                          T.kv[:, 256 * kb:256 * kb + 128], True, True), "sS")
+        dve.wait_ge(S.sS, n["sS"])
+        inc(dve.tensor_reduce(T.nm[0:Q, p:p + 1], T.pa[0:Q, 0:256], AxisListType.X, AluOpType.max, negate=True), "sM")
+        act.wait_ge(S.sM, n["sM"])
+        inc(act.activation(T.pp[0:Q, P0:P0 + 256], T.pa[0:Q, 0:256], ActivationFunctionType.Exp,
+                           bias=T.nm[0:Q, p:p + 1], scale=1.0, accum_out=T.ls[0:Q, p:p + 1]), "sE")
+        pe.wait_ge(S.sE, n["sE"])
+        for kb in range(2):
+            inc(pe.matmul(T.pa[:, 256 + Q * kb:256 + Q * kb + Q], T.pp[0:Q, P0 + 128 * kb:P0 + 128 * kb + 128],
+                          T.ident[0:Q, 0:Q], True, True), "sT")
+        dve.wait_ge(S.sE, n["sE"])
+        inc(dve.reciprocal(T.rs[0:Q, p:p + 1], T.ls[0:Q, p:p + 1]), "sR1")
+        dve.wait_ge(S.sR1, n["sR1"])
+        inc(dve.tensor_scalar(T.rm[0:Q, 4 * p:4 * p + nb], T.mask[0:Q, 0:nb], T.rs[0:Q, p:p + 1], None,
+                              AluOpType.mult), "sR2")
+        act.wait_ge(S.sT, n["sT"])
+        inc(act.activation(T.pt[:, P0:P0 + 2 * Q], T.pa[:, 256:256 + 2 * Q], ActivationFunctionType.Copy), "sC")
+        pe.wait_ge(S.sC, n["sC"])
+        if n.get("sO", 0):
+            pe.wait_ge(S.sO, n["sO"])
+        for b in range(nb):
+            for fb in range(4):
+                for kb in range(2):
+                    inc(pe.matmul(ybank[b][32 * fb:32 * fb + 32, 0:32],
+                                  T.pt[:, P0 + Q * kb + 32 * b:P0 + Q * kb + 32 * b + 32],
+                                  T.kv[:, 256 * kb + 128 + 32 * fb:256 * kb + 128 + 32 * fb + 32],
+                                  kb == 0, kb == 1), "sY%d" % b)
+            if b == 0:
+                pe.wait_ge(S.sR2, n["sR2"])
+                inc(pe.matmul(T.pr[:, 0:nb], T.rep[0:Q, :], T.rm[0:Q, 4 * p:4 * p + nb], True, True), "sRR")
+        dve.wait_ge(S.sRR, n["sRR"])
+        Y0 = 128 * p
+        for b in range(nb):
+            dve.wait_ge(S["sY%d" % b], n["sY%d" % b])
+            inc(dve.tensor_scalar(T.ys[:, Y0 + 32 * b:Y0 + 32 * b + 32], ybank[b][:, 0:32], T.pr[:, b:b + 1], None,
+                                  AluOpType.mult), "sO")
+        if blk == [core]:
+            _store_y([g.sync], T, T.ys[:, Y0:Y0 + 32], S.sO, n["sO"])
+        else:
+            g.wait_ge(S.sO, n["sO"])
+            trs = []
+            for b, c in enumerate(blk):
+                w = place[c][2]
+                m = 0
+                for e in eng[b * w:(b + 1) * w]:
+                    m |= 1 << e
+                cr, cp, _ = topo.addr(c)
+                trs.append(RemoteDMATransfer(dst_ids=[DstId(rid=cr, pnc=cp)], dma_engine_mask=m, remote_sem=S.yarr,
+                                             src=T.ys[:, Y0 + 32 * b:Y0 + 32 * b + 32], dst=T.yl[:, :]))
+                sent += w
+            g.remote_dma_fused(trs, local_sem=S.sent)
+        col += Q
+    g.wait_ge(S.sent, sent)
+    g.wait_ge(S.st, 64)
+
+
+def rank_program(g, core, T, topo):
+    if T.rank_of(core) is None:
+        return
+    plan = _plan(T, topo)
+    if core in plan[0]:
+        _server(g, core, T, topo, plan)
+    else:
+        _client(g, core, T, topo, plan)

@@ -11,29 +11,27 @@ SCRATCH = {
     "qr": ("dram", [2, 128, 32], BF),
     "yl": ("sbuf", [128, 32], BF),
     "kv": ("sbuf", [128, 512], BF),
-    "ql": ("sbuf", [128, 32 * 4 * MAXP], BF),
+    "ql": ("sbuf", [128, 128 * MAXP], BF),
     "ones": ("sbuf", [128, 128], BF),
     "ident": ("sbuf", [128, 128], BF),
-    "ee": ("sbuf", [128, 128], BF),
-    "rep": ("sbuf", [128, 128], BF),
-    "mask": ("sbuf", [128, 4], F32),
     "nm": ("sbuf", [128, 4], F32),
     "ls": ("sbuf", [128, 4], F32),
     "rs": ("sbuf", [128, 4], F32),
-    "rm": ("sbuf", [128, 4 * MAXP], BF),
+    "dg": ("sbuf", [128, 128 * MAXP], BF),
+    "rb": ("sbuf", [128, 128 * MAXP], F32),
     "pp": ("sbuf", [128, 256 * MAXP], BF),
     "pt": ("sbuf", [128, 256 * MAXP], BF),
+    "zt": ("sbuf", [128, 128 * MAXP], BF),
     "ys": ("sbuf", [128, 128 * MAXP], BF),
     "pa": ("psum", [128, 512], F32),
+    "t0": ("psum", [128, 512], F32),
+    "t1": ("psum", [128, 512], F32),
     "pr": ("psum", [128, 512], F32),
-    "y0": ("psum", [128, 512], F32),
-    "y1": ("psum", [128, 512], F32),
-    "y2": ("psum", [128, 512], F32),
-    "y3": ("psum", [128, 512], F32),
+    "yt": ("psum", [128, 512], F32),
 }
 SEMAPHORES = ["ld", "rel0", "rel1", "sent", "yarr", "st", "kvld", "kva", "qa0", "qa1", "qa2",
-              "sA", "sB", "sD", "sF", "sK", "sS", "sM", "sE", "sT", "sC", "sR1", "sR2", "sRR",
-              "sY0", "sY1", "sY2", "sY3", "sO"]
+              "sA", "sB", "sS", "sM", "sE", "sT0", "sT1", "sC0", "sC1", "sR1", "sR2", "sRR", "sRC",
+              "sY", "sZ", "sO"]
 
 
 def _bits(mask):
@@ -69,24 +67,40 @@ def _plan(T, topo):
                       and topo.may_write(x, s)][0]
     passes = {}
     for s in mem:
-        ps = [[s]]
+        ps = []
         for grp in ([c for c in clients if server[c] == s and via[c] is None],
                     [c for c in clients if server[c] == s and via[c] is not None]):
             for i in range(0, len(grp), 4):
                 ps.append(grp[i:i + 4])
         passes[s] = ps
+    full = []
+    for s in mem:
+        if passes[s] and len(passes[s][-1]) < 4:
+            passes[s][-1] = passes[s][-1] + [s]
+        else:
+            full.append(s)
+    for s in full:
+        room = [x for x in mem if x != s and passes[x] and len(passes[x][-1]) < 4
+                and topo.may_write(s, x) and topo.may_write(x, s)]
+        if room:
+            passes[room[0]][-1] = passes[room[0]][-1] + [s]
+            server[s] = room[0]
+            via[s] = None
+        else:
+            passes[s].append([s])
     place = {}
     for s in mem:
         col = 0
-        for i, blk in enumerate(ps_ for ps_ in passes[s]):
+        for i, blk in enumerate(passes[s]):
+            far = [c for c in blk if c != s]
+            w = 0
+            if far:
+                nbits = min(len(_bits(topo.mask(s, c))) for c in far)
+                w = 1
+                while w * 2 * len(far) <= nbits:
+                    w *= 2
             for c in blk:
-                w = 0
-                if c != s:
-                    eng = _bits(topo.mask(s, c))
-                    w = 1
-                    while w * 2 * len(blk) <= len(eng):
-                        w *= 2
-                place[c] = (i, col, w)
+                place[c] = (i, col, w if c != s else 0)
                 col += 32
     return mem, server, via, passes, place
 
@@ -133,6 +147,7 @@ def _server(g, core, T, topo, plan):
     S = T.sem
     pe, dve, act = g.tensor, g.vector, g.scalar
     me = mem.index(core)
+    away = server.get(core)
     n = {}
 
     def inc(instr, name, k=1):
@@ -140,24 +155,20 @@ def _server(g, core, T, topo, plan):
         n[name] = n.get(name, 0) + k
 
     o = 256 * me
+    oi, ocol, ow = place[core]
     g.sync.dma_start(T.kv[:, o:o + 128], T.k[:, :]).then_inc(S.kvld, 16)
     act.dma_start(T.kv[:, o + 128:o + 256], T.v[:, :]).then_inc(S.kvld, 16)
-    g.sync.dma_start(T.ql[:, 0:32], T.q[:, :]).then_inc(S.qa0, 16)
+    if away is None:
+        g.sync.dma_start(T.ql[:, ocol:ocol + 32], T.q[:, :]).then_inc(S["qa%d" % oi], 16)
+    else:
+        g.sync.dma_start(T.qd[:, :], T.q[:, :]).then_inc(S.ld, 16)
 
     inc(dve.memset(T.ones[:, :], 1.0), "sA")
-    inc(dve.memset(T.mask[:, :], 0.0), "sK")
-    dve.wait_ge(S.sK, 1)
-    for b in range(4):
-        inc(dve.memset(T.mask[32 * b:32 * b + 32, b:b + 1], 1.0), "sK")
-    dve.wait_ge(S.sK, 5)
     g.wait_ge(S.sA, 1)
     inc(g.affine_select(T.ident[:, :], T.ones[:, :], [[-1, 128]], AluOpType.is_equal, 0.0, 0, 1), "sB")
-    inc(g.affine_select(T.ee[0:32, :], T.ones[0:32, :], [[0, 4], [-1, 32]], AluOpType.is_equal, 0.0, 0, 1), "sB")
-    pe.wait_ge(S.sB, 2)
-    inc(pe.matmul(T.pr[:, 0:128], T.ee[0:32, :], T.ee[0:32, :], True, True), "sD")
-    dve.wait_ge(S.sD, 1)
-    inc(dve.tensor_copy(T.rep[:, :], T.pr[:, 0:128]), "sF")
-    pe.wait_ge(S.sF, 1)
+    pe.wait_ge(S.sA, 1)
+    pe.wait_ge(S.sB, 1)
+    dve.wait_ge(S.sB, 1)
 
     dsts = [c for ps in passes[core] for c in ps if c != core] + [x for x in mem if x != core]
     common = 0xFFFF
@@ -171,16 +182,23 @@ def _server(g, core, T, topo, plan):
             xr, xp, _ = topo.addr(x)
             g.remote_dma(T.kv[:, o:o + 256], T.kv[:, o:o + 256], S.kva, S.sent, xp, xr, _pick(eng, len(eng)))
             sent += len(eng)
+    if away is not None:
+        xr, xp, _ = topo.addr(away)
+        g.wait_ge(S.ld, 16)
+        g.remote_dma(T.ql[:, ocol:ocol + 32], T.qd[:, :], S["qa%d" % oi], S.sent, xp, xr, _pick(eng, NQ))
+        sent += NQ
     pe.wait_ge(S.kvld, 32)
     pe.wait_ge(S.kva, len(eng) * (len(mem) - 1))
 
-    ybank = [T.y0, T.y1, T.y2, T.y3]
+    tb = [T.t0, T.t1]
     col = 0
     for p, blk in enumerate(passes[core]):
         nb = len(blk)
         Q = 32 * nb
         P0 = 256 * p
-        pe.wait_ge(S["qa%d" % p], 16 if p == 0 else NQ * nb)
+        Y0 = 128 * p
+        far = [c for c in blk if c != core]
+        pe.wait_ge(S["qa%d" % p], NQ * len(far) + 16 * (nb - len(far)))
         for kb in range(2):
             inc(pe.matmul(T.pa[0:Q, 128 * kb:128 * kb + 128], T.ql[:, col:col + Q],
                           T.kv[:, 256 * kb:256 * kb + 128], True, True), "sS")
@@ -191,50 +209,54 @@ def _server(g, core, T, topo, plan):
                            bias=T.nm[0:Q, p:p + 1], scale=1.0, accum_out=T.ls[0:Q, p:p + 1]), "sE")
         pe.wait_ge(S.sE, n["sE"])
         for kb in range(2):
-            inc(pe.matmul(T.pa[:, 256 + Q * kb:256 + Q * kb + Q], T.pp[0:Q, P0 + 128 * kb:P0 + 128 * kb + 128],
-                          T.ident[0:Q, 0:Q], True, True), "sT")
+            inc(pe.matmul(tb[kb][:, 0:Q], T.pp[0:Q, P0 + 128 * kb:P0 + 128 * kb + 128],
+                          T.ident[0:Q, 0:Q], True, True), "sT%d" % kb)
+        for kb in range(2):
+            act.wait_ge(S["sT%d" % kb], n["sT%d" % kb])
+            inc(act.activation(T.pt[:, P0 + Q * kb:P0 + Q * kb + Q], tb[kb][:, 0:Q], ActivationFunctionType.Copy),
+                "sC%d" % kb)
         dve.wait_ge(S.sE, n["sE"])
         inc(dve.reciprocal(T.rs[0:Q, p:p + 1], T.ls[0:Q, p:p + 1]), "sR1")
         dve.wait_ge(S.sR1, n["sR1"])
-        inc(dve.tensor_scalar(T.rm[0:Q, 4 * p:4 * p + nb], T.mask[0:Q, 0:nb], T.rs[0:Q, p:p + 1], None,
-                              AluOpType.mult), "sR2")
-        act.wait_ge(S.sT, n["sT"])
-        inc(act.activation(T.pt[:, P0:P0 + 2 * Q], T.pa[:, 256:256 + 2 * Q], ActivationFunctionType.Copy), "sC")
-        pe.wait_ge(S.sC, n["sC"])
-        if n.get("sO", 0):
-            pe.wait_ge(S.sO, n["sO"])
-        for b in range(nb):
-            for fb in range(4):
-                for kb in range(2):
-                    inc(pe.matmul(ybank[b][32 * fb:32 * fb + 32, 0:32],
-                                  T.pt[:, P0 + Q * kb + 32 * b:P0 + Q * kb + 32 * b + 32],
-                                  T.kv[:, 256 * kb + 128 + 32 * fb:256 * kb + 128 + 32 * fb + 32],
-                                  kb == 0, kb == 1), "sY%d" % b)
-            if b == 0:
-                pe.wait_ge(S.sR2, n["sR2"])
-                inc(pe.matmul(T.pr[:, 0:nb], T.rep[0:Q, :], T.rm[0:Q, 4 * p:4 * p + nb], True, True), "sRR")
+        inc(dve.tensor_scalar(T.dg[0:Q, Y0:Y0 + Q], T.ident[0:Q, 0:Q], T.rs[0:Q, p:p + 1], None, AluOpType.mult), "sR2")
+        pe.wait_ge(S.sC0, n["sC0"])
+        if n.get("sZ", 0):
+            pe.wait_ge(S.sZ, n["sZ"])
+        inc(pe.matmul(T.yt[:, 0:Q], T.kv[:, 128:256], T.pt[:, P0:P0 + Q], True, False), "sY")
+        pe.wait_ge(S.sR2, n["sR2"])
+        if n.get("sRC", 0):
+            pe.wait_ge(S.sRC, n["sRC"])
+        inc(pe.matmul(T.pr[:, 0:Q], T.ones[0:Q, :], T.dg[0:Q, Y0:Y0 + Q], True, True), "sRR")
+        pe.wait_ge(S.sC1, n["sC1"])
+        inc(pe.matmul(T.yt[:, 0:Q], T.kv[:, 384:512], T.pt[:, P0 + Q:P0 + 2 * Q], False, True), "sY")
         dve.wait_ge(S.sRR, n["sRR"])
-        Y0 = 128 * p
-        for b in range(nb):
-            dve.wait_ge(S["sY%d" % b], n["sY%d" % b])
-            inc(dve.tensor_scalar(T.ys[:, Y0 + 32 * b:Y0 + 32 * b + 32], ybank[b][:, 0:32], T.pr[:, b:b + 1], None,
-                                  AluOpType.mult), "sO")
-        if blk == [core]:
-            _store_y([g.sync], T, T.ys[:, Y0:Y0 + 32], S.sO, n["sO"])
-        else:
+        inc(dve.tensor_copy(T.rb[:, Y0:Y0 + Q], T.pr[:, 0:Q]), "sRC")
+        dve.wait_ge(S.sRC, n["sRC"])
+        dve.wait_ge(S.sY, n["sY"])
+        inc(dve.tensor_tensor(T.zt[:, Y0:Y0 + Q], T.yt[:, 0:Q], T.rb[:, Y0:Y0 + Q], AluOpType.mult), "sZ")
+        dve.wait_ge(S.sZ, n["sZ"])
+        inc(dve.transpose(T.ys[:, Y0:Y0 + Q], T.zt[:, Y0:Y0 + Q]), "sO")
+        if far:
             g.wait_ge(S.sO, n["sO"])
             trs = []
             for b, c in enumerate(blk):
+                if c == core:
+                    continue
                 w = place[c][2]
                 m = 0
-                for e in eng[b * w:(b + 1) * w]:
+                for e in eng[len(trs) * w:(len(trs) + 1) * w]:
                     m |= 1 << e
                 cr, cp, _ = topo.addr(c)
                 trs.append(RemoteDMATransfer(dst_ids=[DstId(rid=cr, pnc=cp)], dma_engine_mask=m, remote_sem=S.yarr,
                                              src=T.ys[:, Y0 + 32 * b:Y0 + 32 * b + 32], dst=T.yl[:, :]))
                 sent += w
             g.remote_dma_fused(trs, local_sem=S.sent)
+        if core in blk:
+            b = blk.index(core)
+            _store_y([g.sync], T, T.ys[:, Y0 + 32 * b:Y0 + 32 * b + 32], S.sO, n["sO"])
         col += Q
+    if away is not None:
+        _store_y([g.sync], T, T.yl, S.yarr, ow)
     g.wait_ge(S.sent, sent)
     g.wait_ge(S.st, 64)
 

@@ -12,6 +12,7 @@ SCRATCH = {
     "yl": ("sbuf", [128, 32], BF),
     "kv": ("sbuf", [128, 512], BF),
     "ql": ("sbuf", [128, 128 * MAXP], BF),
+    "zero": ("sbuf", [128, 128], BF),
     "ones": ("sbuf", [128, 128], BF),
     "ident": ("sbuf", [128, 128], BF),
     "nm": ("sbuf", [128, 4], F32),
@@ -30,7 +31,7 @@ SCRATCH = {
     "yt": ("psum", [128, 512], F32),
 }
 SEMAPHORES = ["ld", "rel0", "rel1", "sent", "yarr", "st", "kvld", "kva", "qa0", "qa1", "qa2",
-              "sA", "sB", "sS", "sM", "sE", "sT0", "sT1", "sC0", "sC1", "sR1", "sR2", "sRR", "sRC",
+              "sA0", "sA", "sB", "sS", "sM", "sE", "sT0", "sT1", "sC0", "sC1", "sR1", "sR2", "sRR", "sRC",
               "sY", "sZ", "sO"]
 
 
@@ -65,8 +66,23 @@ def _plan(T, topo):
         else:
             via[c] = [x for x in clients if x != c and topo.chip(x) == topo.chip(c) and server[x] == s
                       and topo.may_write(x, s)][0]
-    passes = {}
+    helpers = []
     for s in mem:
+        early = [c for c in clients if server[c] == s and via[c] is None]
+        late = [c for c in clients if server[c] == s and via[c] is not None]
+        if not (early and late):
+            continue
+        cand = [h for h in range(max(cores) + 1) if T.rank_of(h) is None and h not in helpers
+                and topo.chip(h) == topo.chip(s)
+                and all(topo.may_write(h, c) and topo.may_write(c, h) for c in early)]
+        cand.sort(key=lambda h: topo.die(h) == topo.die(s))
+        if cand:
+            helpers.append(cand[0])
+            for c in early:
+                server[c] = cand[0]
+    servers = mem + helpers
+    passes = {}
+    for s in servers:
         ps = []
         for grp in ([c for c in clients if server[c] == s and via[c] is None],
                     [c for c in clients if server[c] == s and via[c] is not None]):
@@ -89,7 +105,7 @@ def _plan(T, topo):
         else:
             passes[s].append([s])
     place = {}
-    for s in mem:
+    for s in servers:
         col = 0
         for i, blk in enumerate(passes[s]):
             far = [c for c in blk if c != s]
@@ -102,7 +118,19 @@ def _plan(T, topo):
             for c in blk:
                 place[c] = (i, col, w if c != s else 0)
                 col += 32
-    return mem, server, via, passes, place
+    return mem, servers, server, via, passes, place
+
+
+def _kv_split(s, servers, topo):
+    kd = [x for x in servers if x != s]
+    both = topo.mask(s, kd[0])
+    for x in kd:
+        both &= topo.mask(s, x)
+    ab = _bits(both)
+    per = 1
+    while per * 2 * len(kd) <= len(ab):
+        per *= 2
+    return kd, per, [ab[i * per:(i + 1) * per] for i in range(len(kd))]
 
 
 def _store_y(queues, T, src, sem_wait, val):
@@ -114,7 +142,7 @@ def _store_y(queues, T, src, sem_wait, val):
 
 
 def _client(g, core, T, topo, plan):
-    mem, server, via, passes, place = plan
+    mem, servers, server, via, passes, place = plan
     s = server[core]
     rid, pid, _ = topo.addr(s)
     g.sync.dma_start(T.qd[:, :], T.q[:, :]).then_inc(T.sem.ld, 16)
@@ -122,13 +150,15 @@ def _client(g, core, T, topo, plan):
     sent = 0
     if via[core] is None:
         i, col, _w = place[core]
-        m = _pick(_bits(topo.mask(core, s)), NQ)
-        g.remote_dma(T.ql[:, col:col + 32], T.qd[:, :], T.sem["qa%d" % i], T.sem.sent, pid, rid, m)
+        g.remote_dma(T.ql[:, col:col + 32], T.qd[:, :], T.sem["qa%d" % i], T.sem.sent, pid, rid,
+                     _pick(_bits(topo.mask(core, s)), NQ))
         sent += NQ
         for k, c in enumerate([c for c in via if via[c] == core]):
             i, col, _w = place[c]
+            fr, fp, _ = topo.addr(server[c])
             g.wait_ge(T.sem["rel%d" % k], NR)
-            g.remote_dma(T.ql[:, col:col + 32], T.qr[k], T.sem["qa%d" % i], T.sem.sent, pid, rid, m)
+            g.remote_dma(T.ql[:, col:col + 32], T.qr[k], T.sem["qa%d" % i], T.sem.sent, fp, fr,
+                         _pick(_bits(topo.mask(core, server[c])), NQ))
             sent += NQ
     else:
         x = via[core]
@@ -143,10 +173,10 @@ def _client(g, core, T, topo, plan):
 
 
 def _server(g, core, T, topo, plan):
-    mem, server, via, passes, place = plan
+    mem, servers, server, via, passes, place = plan
     S = T.sem
     pe, dve, act = g.tensor, g.vector, g.scalar
-    me = mem.index(core)
+    is_mem = core in mem
     away = server.get(core)
     n = {}
 
@@ -154,44 +184,49 @@ def _server(g, core, T, topo, plan):
         instr.then_inc(S[name], k)
         n[name] = n.get(name, 0) + k
 
-    o = 256 * me
-    oi, ocol, ow = place[core]
-    g.sync.dma_start(T.kv[:, o:o + 128], T.k[:, :]).then_inc(S.kvld, 16)
-    act.dma_start(T.kv[:, o + 128:o + 256], T.v[:, :]).then_inc(S.kvld, 16)
-    if away is None:
-        g.sync.dma_start(T.ql[:, ocol:ocol + 32], T.q[:, :]).then_inc(S["qa%d" % oi], 16)
-    else:
-        g.sync.dma_start(T.qd[:, :], T.q[:, :]).then_inc(S.ld, 16)
+    if is_mem:
+        o = 256 * mem.index(core)
+        oi, ocol, ow = place[core]
+        g.sync.dma_start(T.kv[:, o:o + 128], T.k[:, :]).then_inc(S.kvld, 16)
+        act.dma_start(T.kv[:, o + 128:o + 256], T.v[:, :]).then_inc(S.kvld, 16)
+        if away is None:
+            g.sync.dma_start(T.ql[:, ocol:ocol + 32], T.q[:, :]).then_inc(S["qa%d" % oi], 16)
+        else:
+            g.sync.dma_start(T.qd[:, :], T.q[:, :]).then_inc(S.ld, 16)
 
-    inc(dve.memset(T.ones[:, :], 1.0), "sA")
-    g.wait_ge(S.sA, 1)
-    inc(g.affine_select(T.ident[:, :], T.ones[:, :], [[-1, 128]], AluOpType.is_equal, 0.0, 0, 1), "sB")
-    pe.wait_ge(S.sA, 1)
-    pe.wait_ge(S.sB, 1)
-    dve.wait_ge(S.sB, 1)
+    inc(dve.memset(T.zero[:, :], 0.0), "sA0")
+    act.wait_ge(S.sA0, 1)
+    inc(act.activation(T.ones[:, :], T.zero[:, :], ActivationFunctionType.Exp), "sA")
 
-    dsts = [c for ps in passes[core] for c in ps if c != core] + [x for x in mem if x != core]
-    common = 0xFFFF
+    dsts = [c for ps in passes[core] for c in ps if c != core] + ([away] if away is not None else [])
+    common = topo.mask(core, dsts[0])
     for d in dsts:
         common &= topo.mask(core, d)
     eng = _bits(common)
     sent = 0
-    g.wait_ge(S.kvld, 32)
-    for x in mem:
-        if x != core:
+    if is_mem:
+        kd, per, sets = _kv_split(core, servers, topo)
+        trs = []
+        for x, es in zip(kd, sets):
             xr, xp, _ = topo.addr(x)
-            g.remote_dma(T.kv[:, o:o + 256], T.kv[:, o:o + 256], S.kva, S.sent, xp, xr, _pick(eng, len(eng)))
-            sent += len(eng)
-    if away is not None:
-        xr, xp, _ = topo.addr(away)
-        g.wait_ge(S.ld, 16)
-        g.remote_dma(T.ql[:, ocol:ocol + 32], T.qd[:, :], S["qa%d" % oi], S.sent, xp, xr, _pick(eng, NQ))
-        sent += NQ
-    pe.wait_ge(S.kvld, 32)
-    pe.wait_ge(S.kva, len(eng) * (len(mem) - 1))
+            trs.append(RemoteDMATransfer(dst_ids=[DstId(rid=xr, pnc=xp)], dma_engine_mask=_pick(es, len(es)),
+                                         remote_sem=S.kva, src=T.kv[:, o:o + 256], dst=T.kv[:, o:o + 256]))
+            sent += per
+        g.wait_ge(S.kvld, 32)
+        g.remote_dma_fused(trs, local_sem=S.sent)
+        if away is not None:
+            xr, xp, _ = topo.addr(away)
+            g.wait_ge(S.ld, 16)
+            g.remote_dma(T.ql[:, ocol:ocol + 32], T.qd[:, :], S["qa%d" % oi], S.sent, xp, xr, _pick(eng, NQ))
+            sent += NQ
+        pe.wait_ge(S.kvld, 32)
+    g.wait_ge(S.sA, 1)
+    inc(g.affine_select(T.ident[:, :], T.ones[:, :], [[-1, 128]], AluOpType.is_equal, 0.0, 0, 1), "sB")
+    pe.wait_ge(S.kva, sum(_kv_split(x, servers, topo)[1] for x in mem if x != core))
 
     tb = [T.t0, T.t1]
     col = 0
+    stores = 0
     for p, blk in enumerate(passes[core]):
         nb = len(blk)
         Q = 32 * nb
@@ -208,6 +243,10 @@ def _server(g, core, T, topo, plan):
         inc(act.activation(T.pp[0:Q, P0:P0 + 256], T.pa[0:Q, 0:256], ActivationFunctionType.Exp,
                            bias=T.nm[0:Q, p:p + 1], scale=1.0, accum_out=T.ls[0:Q, p:p + 1]), "sE")
         pe.wait_ge(S.sE, n["sE"])
+        if p == 0:
+            pe.wait_ge(S.sA, 1)
+            pe.wait_ge(S.sB, 1)
+            dve.wait_ge(S.sB, 1)
         for kb in range(2):
             inc(pe.matmul(tb[kb][:, 0:Q], T.pp[0:Q, P0 + 128 * kb:P0 + 128 * kb + 128],
                           T.ident[0:Q, 0:Q], True, True), "sT%d" % kb)
@@ -254,18 +293,21 @@ def _server(g, core, T, topo, plan):
         if core in blk:
             b = blk.index(core)
             _store_y([g.sync], T, T.ys[:, Y0 + 32 * b:Y0 + 32 * b + 32], S.sO, n["sO"])
+            stores += 64
         col += Q
     if away is not None:
         _store_y([g.sync], T, T.yl, S.yarr, ow)
+        stores += 64
     g.wait_ge(S.sent, sent)
-    g.wait_ge(S.st, 64)
+    if stores:
+        g.wait_ge(S.st, stores)
 
 
 def rank_program(g, core, T, topo):
-    if T.rank_of(core) is None:
-        return
     plan = _plan(T, topo)
-    if core in plan[0]:
+    if T.rank_of(core) is None and core not in plan[1]:
+        return
+    if core in plan[1]:
         _server(g, core, T, topo, plan)
     else:
         _client(g, core, T, topo, plan)

@@ -13,26 +13,27 @@ SCRATCH = {
     "kv": ("sbuf", [128, 512], BF),
     "ql": ("sbuf", [128, 128 * MAXP], BF),
     "zero": ("sbuf", [128, 128], BF),
-    "ones": ("sbuf", [128, 128], BF),
     "ident": ("sbuf", [128, 128], BF),
+    "rr": ("sbuf", [128, 128], BF),
+    "ee": ("sbuf", [128, 128], BF),
+    "mk": ("sbuf", [128, 8], BF),
+    "mr": ("sbuf", [128, 8 * MAXP], BF),
     "nm": ("sbuf", [128, 4], F32),
     "ls": ("sbuf", [128, 4], F32),
     "rs": ("sbuf", [128, 4], F32),
-    "dg": ("sbuf", [128, 128 * MAXP], BF),
-    "rb": ("sbuf", [128, 128 * MAXP], F32),
     "pp": ("sbuf", [128, 256 * MAXP], BF),
     "pt": ("sbuf", [128, 256 * MAXP], BF),
-    "zt": ("sbuf", [128, 128 * MAXP], BF),
     "ys": ("sbuf", [128, 128 * MAXP], BF),
     "pa": ("psum", [128, 512], F32),
     "t0": ("psum", [128, 512], F32),
     "t1": ("psum", [128, 512], F32),
     "pr": ("psum", [128, 512], F32),
     "yt": ("psum", [128, 512], F32),
+    "ep": ("psum", [128, 512], F32),
 }
-SEMAPHORES = ["ld", "rel0", "rel1", "sent", "yarr", "st", "kvld", "kva", "qa0", "qa1", "qa2",
-              "sA0", "sA", "sB", "sS", "sM", "sE", "sT0", "sT1", "sC0", "sC1", "sR1", "sR2", "sRR", "sRC",
-              "sY", "sZ", "sO"]
+SEMAPHORES = ["ld", "rel0", "rel1", "sent", "yarr", "st", "kld", "vld", "ka", "va", "qa0", "qa1", "qa2",
+              "sA0", "sA", "sB", "sRr", "sEp", "sEE", "sS", "sM", "sE", "sT0", "sT1", "sC0", "sC1", "sR1", "sR2",
+              "sRR", "sY", "sO"]
 
 
 def _bits(mask):
@@ -74,12 +75,18 @@ def _plan(T, topo):
             continue
         cand = [h for h in range(max(cores) + 1) if T.rank_of(h) is None and h not in helpers
                 and topo.chip(h) == topo.chip(s)
-                and all(topo.may_write(h, c) and topo.may_write(c, h) for c in early)]
+                and all(topo.may_write(h, c) for c in early + late) and all(topo.may_write(c, h) for c in early)
+                and all(topo.may_write(via[c], h) for c in late)]
         cand.sort(key=lambda h: topo.die(h) == topo.die(s))
-        if cand:
-            helpers.append(cand[0])
-            for c in early:
-                server[c] = cand[0]
+        for size in (2, 4):
+            groups = [late[i:i + size] for i in range(0, len(late), size)][1:] \
+                + [early[i:i + size] for i in range(0, len(early), size)]
+            if len(groups) <= len(cand):
+                for h, grp in zip(cand, groups):
+                    helpers.append(h)
+                    for c in grp:
+                        server[c] = h
+                break
     servers = mem + helpers
     passes = {}
     for s in servers:
@@ -121,16 +128,28 @@ def _plan(T, topo):
     return mem, servers, server, via, passes, place
 
 
+def _split(bits, k):
+    per = 1
+    while per * 2 * k <= len(bits):
+        per *= 2
+    return per, [bits[i * per:(i + 1) * per] for i in range(k)]
+
+
 def _kv_split(s, servers, topo):
     kd = [x for x in servers if x != s]
     both = topo.mask(s, kd[0])
     for x in kd:
         both &= topo.mask(s, x)
-    ab = _bits(both)
-    per = 1
-    while per * 2 * len(kd) <= len(ab):
-        per *= 2
-    return kd, per, [ab[i * per:(i + 1) * per] for i in range(len(kd))]
+    per, sets = _split(_bits(both), len(kd))
+    return kd, per, sets
+
+
+def _y_engines(s, server, passes, topo):
+    dsts = [c for ps in passes[s] for c in ps if c != s] + ([server[s]] if s in server else [])
+    common = topo.mask(s, dsts[0])
+    for d in dsts:
+        common &= topo.mask(s, d)
+    return _bits(common)
 
 
 def _store_y(queues, T, src, sem_wait, val):
@@ -178,6 +197,7 @@ def _server(g, core, T, topo, plan):
     pe, dve, act = g.tensor, g.vector, g.scalar
     is_mem = core in mem
     away = server.get(core)
+    maker = servers[len(mem)] if len(servers) > len(mem) else None
     n = {}
 
     def inc(instr, name, k=1):
@@ -187,42 +207,65 @@ def _server(g, core, T, topo, plan):
     if is_mem:
         o = 256 * mem.index(core)
         oi, ocol, ow = place[core]
-        g.sync.dma_start(T.kv[:, o:o + 128], T.k[:, :]).then_inc(S.kvld, 16)
-        act.dma_start(T.kv[:, o + 128:o + 256], T.v[:, :]).then_inc(S.kvld, 16)
         if away is None:
+            g.sync.dma_start(T.kv[:, o:o + 128], T.k[:, :]).then_inc(S.kld, 16)
+            act.dma_start(T.kv[:, o + 128:o + 256], T.v[:, :]).then_inc(S.vld, 16)
             g.sync.dma_start(T.ql[:, ocol:ocol + 32], T.q[:, :]).then_inc(S["qa%d" % oi], 16)
         else:
             g.sync.dma_start(T.qd[:, :], T.q[:, :]).then_inc(S.ld, 16)
+            act.dma_start(T.kv[:, o:o + 128], T.k[:, :]).then_inc(S.kld, 16)
+            g.sync.dma_start(T.kv[:, o + 128:o + 256], T.v[:, :]).then_inc(S.vld, 16)
 
     inc(dve.memset(T.zero[:, :], 0.0), "sA0")
-    act.wait_ge(S.sA0, 1)
-    inc(act.activation(T.ones[:, :], T.zero[:, :], ActivationFunctionType.Exp), "sA")
+    inc(dve.memset(T.mk[:, :], 0.0), "sA0")
+    act.wait_ge(S.sA0, 2)
+    for b in range(4):
+        inc(act.activation(T.mk[32 * b:32 * b + 32, b:b + 1], T.zero[32 * b:32 * b + 32, 0:1],
+                           ActivationFunctionType.Exp), "sA")
 
-    dsts = [c for ps in passes[core] for c in ps if c != core] + ([away] if away is not None else [])
-    common = topo.mask(core, dsts[0])
-    for d in dsts:
-        common &= topo.mask(core, d)
-    eng = _bits(common)
+    eng = _y_engines(core, server, passes, topo)
     sent = 0
+    g.wait_ge(S.sA0, 2)
+    if maker is None or not is_mem:
+        inc(g.affine_select(T.ident[:, :], T.zero[:, :], [[-1, 128]], AluOpType.not_equal, 1.0, 0, 1), "sB")
+        n_ident = 1
+    if maker is not None:
+        wi, sets = _split(_y_engines(maker, server, passes, topo), len(mem))
+        if core == maker:
+            trs = []
+            for x, es in zip(mem, sets):
+                xr, xp, _ = topo.addr(x)
+                trs.append(RemoteDMATransfer(dst_ids=[DstId(rid=xr, pnc=xp)], dma_engine_mask=_pick(es, wi),
+                                             remote_sem=S.sB, src=T.ident[:, :], dst=T.ident[:, :]))
+                sent += wi
+            g.wait_ge(S.sB, 1)
+            g.remote_dma_fused(trs, local_sem=S.sent)
+        elif is_mem:
+            n_ident = wi
+    inc(g.affine_select(T.rr[0:32, :], T.zero[0:32, :], [[0, 4], [-1, 32]], AluOpType.not_equal, 1.0, 0, 1), "sRr")
+    pe.wait_ge(S.sRr, 1)
+    inc(pe.matmul(T.ep[:, 0:128], T.rr[0:32, :], T.rr[0:32, :], True, True), "sEp")
+    dve.wait_ge(S.sEp, 1)
+    inc(dve.tensor_copy(T.ee[:, :], T.ep[:, 0:128]), "sEE")
     if is_mem:
-        kd, per, sets = _kv_split(core, servers, topo)
-        trs = []
-        for x, es in zip(kd, sets):
-            xr, xp, _ = topo.addr(x)
-            trs.append(RemoteDMATransfer(dst_ids=[DstId(rid=xr, pnc=xp)], dma_engine_mask=_pick(es, len(es)),
-                                         remote_sem=S.kva, src=T.kv[:, o:o + 256], dst=T.kv[:, o:o + 256]))
-            sent += per
-        g.wait_ge(S.kvld, 32)
-        g.remote_dma_fused(trs, local_sem=S.sent)
         if away is not None:
             xr, xp, _ = topo.addr(away)
             g.wait_ge(S.ld, 16)
             g.remote_dma(T.ql[:, ocol:ocol + 32], T.qd[:, :], S["qa%d" % oi], S.sent, xp, xr, _pick(eng, NQ))
             sent += NQ
-        pe.wait_ge(S.kvld, 32)
-    g.wait_ge(S.sA, 1)
-    inc(g.affine_select(T.ident[:, :], T.ones[:, :], [[-1, 128]], AluOpType.is_equal, 0.0, 0, 1), "sB")
-    pe.wait_ge(S.kva, sum(_kv_split(x, servers, topo)[1] for x in mem if x != core))
+        kd, per, sets = _kv_split(core, servers, topo)
+        for lsem, asem, c0 in ((S.kld, S.ka, o), (S.vld, S.va, o + 128)):
+            trs = []
+            for x, es in zip(kd, sets):
+                xr, xp, _ = topo.addr(x)
+                trs.append(RemoteDMATransfer(dst_ids=[DstId(rid=xr, pnc=xp)], dma_engine_mask=_pick(es, per),
+                                             remote_sem=asem, src=T.kv[:, c0:c0 + 128], dst=T.kv[:, c0:c0 + 128]))
+                sent += per
+            g.wait_ge(lsem, 16)
+            g.remote_dma_fused(trs, local_sem=S.sent)
+        pe.wait_ge(S.kld, 16)
+    n_kv = sum(_kv_split(x, servers, topo)[1] for x in mem if x != core)
+    pe.wait_ge(S.ka, n_kv)
 
     tb = [T.t0, T.t1]
     col = 0
@@ -244,9 +287,7 @@ def _server(g, core, T, topo, plan):
                            bias=T.nm[0:Q, p:p + 1], scale=1.0, accum_out=T.ls[0:Q, p:p + 1]), "sE")
         pe.wait_ge(S.sE, n["sE"])
         if p == 0:
-            pe.wait_ge(S.sA, 1)
-            pe.wait_ge(S.sB, 1)
-            dve.wait_ge(S.sB, 1)
+            pe.wait_ge(S.sB, n_ident)
         for kb in range(2):
             inc(pe.matmul(tb[kb][:, 0:Q], T.pp[0:Q, P0 + 128 * kb:P0 + 128 * kb + 128],
                           T.ident[0:Q, 0:Q], True, True), "sT%d" % kb)
@@ -257,24 +298,34 @@ def _server(g, core, T, topo, plan):
         dve.wait_ge(S.sE, n["sE"])
         inc(dve.reciprocal(T.rs[0:Q, p:p + 1], T.ls[0:Q, p:p + 1]), "sR1")
         dve.wait_ge(S.sR1, n["sR1"])
-        inc(dve.tensor_scalar(T.dg[0:Q, Y0:Y0 + Q], T.ident[0:Q, 0:Q], T.rs[0:Q, p:p + 1], None, AluOpType.mult), "sR2")
-        pe.wait_ge(S.sC0, n["sC0"])
-        if n.get("sZ", 0):
-            pe.wait_ge(S.sZ, n["sZ"])
-        inc(pe.matmul(T.yt[:, 0:Q], T.kv[:, 128:256], T.pt[:, P0:P0 + Q], True, False), "sY")
+        if p == 0:
+            dve.wait_ge(S.sA, 4)
+        inc(dve.tensor_scalar(T.mr[0:Q, 8 * p:8 * p + nb], T.mk[0:Q, 0:nb], T.rs[0:Q, p:p + 1], None,
+                              AluOpType.mult), "sR2")
+        if p == 0:
+            pe.wait_ge(S.sEE, 1)
+        if n.get("sO", 0):
+            pe.wait_ge(S.sO, n["sO"])
         pe.wait_ge(S.sR2, n["sR2"])
-        if n.get("sRC", 0):
-            pe.wait_ge(S.sRC, n["sRC"])
-        inc(pe.matmul(T.pr[:, 0:Q], T.ones[0:Q, :], T.dg[0:Q, Y0:Y0 + Q], True, True), "sRR")
+        inc(pe.matmul(T.pr[:, 0:nb], T.ee[0:Q, :], T.mr[0:Q, 8 * p:8 * p + nb], True, True), "sRR")
+        if p == 0:
+            if is_mem:
+                pe.wait_ge(S.vld, 16)
+            pe.wait_ge(S.va, n_kv)
+        pe.wait_ge(S.sC0, n["sC0"])
         pe.wait_ge(S.sC1, n["sC1"])
-        inc(pe.matmul(T.yt[:, 0:Q], T.kv[:, 384:512], T.pt[:, P0 + Q:P0 + 2 * Q], False, True), "sY")
+        for b in range(nb):
+            for fb in range(4):
+                for kb in range(2):
+                    inc(pe.matmul(T.yt[32 * fb:32 * fb + 32, 32 * b:32 * b + 32],
+                                  T.pt[:, P0 + Q * kb + 32 * b:P0 + Q * kb + 32 * b + 32],
+                                  T.kv[:, 256 * kb + 128 + 32 * fb:256 * kb + 128 + 32 * fb + 32],
+                                  kb == 0, kb == 1), "sY")
         dve.wait_ge(S.sRR, n["sRR"])
-        inc(dve.tensor_copy(T.rb[:, Y0:Y0 + Q], T.pr[:, 0:Q]), "sRC")
-        dve.wait_ge(S.sRC, n["sRC"])
         dve.wait_ge(S.sY, n["sY"])
-        inc(dve.tensor_tensor(T.zt[:, Y0:Y0 + Q], T.yt[:, 0:Q], T.rb[:, Y0:Y0 + Q], AluOpType.mult), "sZ")
-        dve.wait_ge(S.sZ, n["sZ"])
-        inc(dve.transpose(T.ys[:, Y0:Y0 + Q], T.zt[:, Y0:Y0 + Q]), "sO")
+        for b in range(nb):
+            inc(dve.tensor_scalar(T.ys[:, Y0 + 32 * b:Y0 + 32 * b + 32], T.yt[:, 32 * b:32 * b + 32],
+                                  T.pr[:, b:b + 1], None, AluOpType.mult), "sO")
         if far:
             g.wait_ge(S.sO, n["sO"])
             trs = []

@@ -3,7 +3,6 @@ from concourse.mybir import AluOpType, AxisListType, ActivationFunctionType
 
 NQ = 8
 NR = 2
-MAXP = 3
 BF, F32 = "bfloat16", "float32"
 
 SCRATCH = {
@@ -11,29 +10,30 @@ SCRATCH = {
     "qr": ("dram", [2, 128, 32], BF),
     "yl": ("sbuf", [128, 32], BF),
     "kv": ("sbuf", [128, 512], BF),
-    "ql": ("sbuf", [128, 128 * MAXP], BF),
+    "ql": ("sbuf", [128, 128], BF),
     "zero": ("sbuf", [128, 128], BF),
     "ident": ("sbuf", [128, 128], BF),
     "rr": ("sbuf", [128, 128], BF),
     "ee": ("sbuf", [128, 128], BF),
     "mk": ("sbuf", [128, 8], BF),
-    "mr": ("sbuf", [128, 8 * MAXP], BF),
+    "mr": ("sbuf", [128, 8], BF),
     "nm": ("sbuf", [128, 4], F32),
     "ls": ("sbuf", [128, 4], F32),
     "rs": ("sbuf", [128, 4], F32),
-    "pp": ("sbuf", [128, 256 * MAXP], BF),
-    "pt": ("sbuf", [128, 256 * MAXP], BF),
-    "ys": ("sbuf", [128, 128 * MAXP], BF),
+    "pp": ("sbuf", [128, 256], BF),
+    "pt": ("sbuf", [128, 256], BF),
+    "ys": ("sbuf", [128, 96], BF),
     "pa": ("psum", [128, 512], F32),
     "t0": ("psum", [128, 512], F32),
     "t1": ("psum", [128, 512], F32),
-    "pr": ("psum", [128, 512], F32),
-    "yt": ("psum", [128, 512], F32),
+    "z0": ("psum", [128, 512], F32),
+    "z1": ("psum", [128, 512], F32),
+    "z2": ("psum", [128, 512], F32),
     "ep": ("psum", [128, 512], F32),
 }
-SEMAPHORES = ["ld", "rel0", "rel1", "sent", "yarr", "st", "kld", "vld", "ka", "va", "qa0", "qa1", "qa2",
-              "sA0", "sA", "sB", "sRr", "sEp", "sEE", "sS", "sM", "sE", "sT0", "sT1", "sC0", "sC1", "sR1", "sR2",
-              "sRR", "sY", "sO"]
+SEMAPHORES = ["ld", "rel0", "rel1", "sent", "yarr", "st", "kld", "vld", "ka", "va", "qa",
+              "sA0", "sA", "sB", "sRr", "sEp", "sEE", "sS", "sM", "sE", "sTa", "sTb", "sC", "sRa", "sRb", "sP",
+              "sY0", "sY1", "sY2", "sO0", "sO1", "sO2"]
 
 
 def _bits(mask):
@@ -48,91 +48,40 @@ def _pick(bits, n):
     return m
 
 
-def _plan(T, topo):
-    cores = list(T.cores)
-    mem = [cores[j] for j in T.tables["MEM"]]
-    clients = [c for c in cores if c not in mem]
-    opts = {c: [s for s in mem if topo.may_write(s, c)] for c in clients}
-    load = {s: 1 for s in mem}
-    server = {}
-    for c in sorted(clients, key=lambda c: len(opts[c])):
-        s = min(opts[c], key=lambda x: load[x])
-        server[c] = s
-        load[s] += 1
-    via = {}
-    for c in clients:
-        s = server[c]
-        if topo.may_write(c, s):
-            via[c] = None
-        else:
-            via[c] = [x for x in clients if x != c and topo.chip(x) == topo.chip(c) and server[x] == s
-                      and topo.may_write(x, s)][0]
-    helpers = []
-    for s in mem:
-        early = [c for c in clients if server[c] == s and via[c] is None]
-        late = [c for c in clients if server[c] == s and via[c] is not None]
-        if not (early and late):
-            continue
-        cand = [h for h in range(max(cores) + 1) if T.rank_of(h) is None and h not in helpers
-                and topo.chip(h) == topo.chip(s)
-                and all(topo.may_write(h, c) for c in early + late) and all(topo.may_write(c, h) for c in early)
-                and all(topo.may_write(via[c], h) for c in late)]
-        cand.sort(key=lambda h: topo.die(h) == topo.die(s))
-        for size in (2, 4):
-            groups = [late[i:i + size] for i in range(0, len(late), size)][1:] \
-                + [early[i:i + size] for i in range(0, len(early), size)]
-            if len(groups) <= len(cand):
-                for h, grp in zip(cand, groups):
-                    helpers.append(h)
-                    for c in grp:
-                        server[c] = h
-                break
-    servers = mem + helpers
-    passes = {}
-    for s in servers:
-        ps = []
-        for grp in ([c for c in clients if server[c] == s and via[c] is None],
-                    [c for c in clients if server[c] == s and via[c] is not None]):
-            for i in range(0, len(grp), 4):
-                ps.append(grp[i:i + 4])
-        passes[s] = ps
-    full = []
-    for s in mem:
-        if passes[s] and len(passes[s][-1]) < 4:
-            passes[s][-1] = passes[s][-1] + [s]
-        else:
-            full.append(s)
-    for s in full:
-        room = [x for x in mem if x != s and passes[x] and len(passes[x][-1]) < 4
-                and topo.may_write(s, x) and topo.may_write(x, s)]
-        if room:
-            passes[room[0]][-1] = passes[room[0]][-1] + [s]
-            server[s] = room[0]
-            via[s] = None
-        else:
-            passes[s].append([s])
-    place = {}
-    for s in servers:
-        col = 0
-        for i, blk in enumerate(passes[s]):
-            far = [c for c in blk if c != s]
-            w = 0
-            if far:
-                nbits = min(len(_bits(topo.mask(s, c))) for c in far)
-                w = 1
-                while w * 2 * len(far) <= nbits:
-                    w *= 2
-            for c in blk:
-                place[c] = (i, col, w if c != s else 0)
-                col += 32
-    return mem, servers, server, via, passes, place
-
-
 def _split(bits, k):
     per = 1
     while per * 2 * k <= len(bits):
         per *= 2
     return per, [bits[i * per:(i + 1) * per] for i in range(k)]
+
+
+def _plan(T, topo):
+    cores = list(T.cores)
+    mem = [cores[j] for j in T.tables["MEM"]]
+    clients = [c for c in cores if c not in mem]
+    home = topo.chip(mem[0])
+    easy = [c for c in clients if all(topo.may_write(s, c) for s in mem)]
+    hard = [c for c in clients if c not in easy]
+    ports = [h for h in range(max(cores) + 1) if topo.chip(h) == home and (h in mem or T.rank_of(h) is None)
+             and all(topo.may_write(h, c) for c in hard)]
+    pmem = [s for s in ports if s in mem]
+    helpers = sorted([h for h in ports if h not in mem], key=lambda h: topo.die(h) == topo.die(pmem[0]))
+    early = [c for c in hard if topo.may_write(c, ports[0])]
+    late = [c for c in hard if c not in early]
+    via = {c: None for c in clients}
+    for c in late:
+        via[c] = [x for x in early if topo.chip(x) == topo.chip(c)][0]
+    servers = mem + helpers
+    blocks = {s: [] for s in servers}
+    groups = [late[i:i + 2] for i in range(0, len(late), 2)] + [early[i:i + 2] for i in range(0, len(early), 2)]
+    for h, grp in zip(pmem[:1] + helpers, groups):
+        blocks[h] = list(grp)
+    plain = [s for s in mem if not blocks[s]] or mem
+    blocks[plain[0]] = blocks[plain[0]] + easy
+    for s in mem:
+        blocks[s] = blocks[s] + [s]
+    server = {c: s for s in servers for c in blocks[s]}
+    return mem, helpers, servers, server, via, blocks
 
 
 def _kv_split(s, servers, topo):
@@ -144,12 +93,16 @@ def _kv_split(s, servers, topo):
     return kd, per, sets
 
 
-def _y_engines(s, server, passes, topo):
-    dsts = [c for ps in passes[s] for c in ps if c != s] + ([server[s]] if s in server else [])
+def _y_engines(s, blocks, topo):
+    dsts = [c for c in blocks[s] if c != s]
     common = topo.mask(s, dsts[0])
     for d in dsts:
         common &= topo.mask(s, d)
     return _bits(common)
+
+
+def _jobs(mem, helpers):
+    return dict(zip(helpers, [("ident", list(mem))] + [("ee", [m]) for m in mem]))
 
 
 def _store_y(queues, T, src, sem_wait, val):
@@ -161,23 +114,24 @@ def _store_y(queues, T, src, sem_wait, val):
 
 
 def _client(g, core, T, topo, plan):
-    mem, servers, server, via, passes, place = plan
-    s = server[core]
-    rid, pid, _ = topo.addr(s)
+    mem, helpers, servers, server, via, blocks = plan
     g.sync.dma_start(T.qd[:, :], T.q[:, :]).then_inc(T.sem.ld, 16)
     g.wait_ge(T.sem.ld, 16)
     sent = 0
-    if via[core] is None:
-        i, col, _w = place[core]
-        g.remote_dma(T.ql[:, col:col + 32], T.qd[:, :], T.sem["qa%d" % i], T.sem.sent, pid, rid,
+
+    def to_server(c, src):
+        s = server[c]
+        rid, pid, _ = topo.addr(s)
+        col = 32 * blocks[s].index(c)
+        g.remote_dma(T.ql[:, col:col + 32], src, T.sem.qa, T.sem.sent, pid, rid,
                      _pick(_bits(topo.mask(core, s)), NQ))
+
+    if via[core] is None:
+        to_server(core, T.qd[:, :])
         sent += NQ
         for k, c in enumerate([c for c in via if via[c] == core]):
-            i, col, _w = place[c]
-            fr, fp, _ = topo.addr(server[c])
             g.wait_ge(T.sem["rel%d" % k], NR)
-            g.remote_dma(T.ql[:, col:col + 32], T.qr[k], T.sem["qa%d" % i], T.sem.sent, fp, fr,
-                         _pick(_bits(topo.mask(core, server[c])), NQ))
+            to_server(c, T.qr[k])
             sent += NQ
     else:
         x = via[core]
@@ -186,73 +140,46 @@ def _client(g, core, T, topo, plan):
         g.remote_dma(T.qr[k], T.qd[:, :], T.sem["rel%d" % k], T.sem.sent, xp, xr,
                      _pick(_bits(topo.mask(core, x)), NR))
         sent += NR
-    _store_y([g.sync, g.scalar], T, T.yl, T.sem.yarr, place[core][2])
+    _store_y([g.sync, g.scalar], T, T.yl, T.sem.yarr, len(_y_engines(server[core], blocks, topo)))
     g.wait_ge(T.sem.sent, sent)
     g.wait_ge(T.sem.st, 64)
 
 
 def _server(g, core, T, topo, plan):
-    mem, servers, server, via, passes, place = plan
+    mem, helpers, servers, server, via, blocks = plan
     S = T.sem
     pe, dve, act = g.tensor, g.vector, g.scalar
     is_mem = core in mem
-    away = server.get(core)
-    maker = servers[len(mem)] if len(servers) > len(mem) else None
-    n = {}
-
-    def inc(instr, name, k=1):
-        instr.then_inc(S[name], k)
-        n[name] = n.get(name, 0) + k
+    blk = blocks[core]
+    nb = len(blk)
+    Q = 32 * nb
+    nfar = len([c for c in blk if c != core])
+    EXP, COPY = ActivationFunctionType.Exp, ActivationFunctionType.Copy
+    MUL = AluOpType.mult
+    TB, Z = [T.t0, T.t1], [T.z0, T.z1, T.z2]
 
     if is_mem:
         o = 256 * mem.index(core)
-        oi, ocol, ow = place[core]
-        if away is None:
-            g.sync.dma_start(T.kv[:, o:o + 128], T.k[:, :]).then_inc(S.kld, 16)
-            act.dma_start(T.kv[:, o + 128:o + 256], T.v[:, :]).then_inc(S.vld, 16)
-            g.sync.dma_start(T.ql[:, ocol:ocol + 32], T.q[:, :]).then_inc(S["qa%d" % oi], 16)
-        else:
-            g.sync.dma_start(T.qd[:, :], T.q[:, :]).then_inc(S.ld, 16)
-            act.dma_start(T.kv[:, o:o + 128], T.k[:, :]).then_inc(S.kld, 16)
-            g.sync.dma_start(T.kv[:, o + 128:o + 256], T.v[:, :]).then_inc(S.vld, 16)
+        ocol = 32 * blk.index(core)
+        g.sync.dma_start(T.kv[:, o:o + 128], T.k[:, :]).then_inc(S.kld, 16)
+        act.dma_start(T.kv[:, o + 128:o + 256], T.v[:, :]).then_inc(S.vld, 16)
+        g.sync.dma_start(T.ql[:, ocol:ocol + 32], T.q[:, :]).then_inc(S.qa, 16)
 
-    inc(dve.memset(T.zero[:, :], 0.0), "sA0")
-    inc(dve.memset(T.mk[:, :], 0.0), "sA0")
+    dve.memset(T.zero[:, :], 0.0).then_inc(S.sA0, 1)
+    dve.memset(T.mk[:, :], 0.0).then_inc(S.sA0, 1)
     act.wait_ge(S.sA0, 2)
     for b in range(4):
-        inc(act.activation(T.mk[32 * b:32 * b + 32, b:b + 1], T.zero[32 * b:32 * b + 32, 0:1],
-                           ActivationFunctionType.Exp), "sA")
+        act.activation(T.mk[32 * b:32 * b + 32, b:b + 1], T.zero[32 * b:32 * b + 32, 0:1], EXP).then_inc(S.sA, 1)
 
-    eng = _y_engines(core, server, passes, topo)
+    eng = _y_engines(core, blocks, topo)
+    jobs = _jobs(mem, helpers)
     sent = 0
-    g.wait_ge(S.sA0, 2)
-    if maker is None or not is_mem:
-        inc(g.affine_select(T.ident[:, :], T.zero[:, :], [[-1, 128]], AluOpType.not_equal, 1.0, 0, 1), "sB")
-        n_ident = 1
-    if maker is not None:
-        wi, sets = _split(_y_engines(maker, server, passes, topo), len(mem))
-        if core == maker:
-            trs = []
-            for x, es in zip(mem, sets):
-                xr, xp, _ = topo.addr(x)
-                trs.append(RemoteDMATransfer(dst_ids=[DstId(rid=xr, pnc=xp)], dma_engine_mask=_pick(es, wi),
-                                             remote_sem=S.sB, src=T.ident[:, :], dst=T.ident[:, :]))
-                sent += wi
-            g.wait_ge(S.sB, 1)
-            g.remote_dma_fused(trs, local_sem=S.sent)
-        elif is_mem:
-            n_ident = wi
-    inc(g.affine_select(T.rr[0:32, :], T.zero[0:32, :], [[0, 4], [-1, 32]], AluOpType.not_equal, 1.0, 0, 1), "sRr")
-    pe.wait_ge(S.sRr, 1)
-    inc(pe.matmul(T.ep[:, 0:128], T.rr[0:32, :], T.rr[0:32, :], True, True), "sEp")
-    dve.wait_ge(S.sEp, 1)
-    inc(dve.tensor_copy(T.ee[:, :], T.ep[:, 0:128]), "sEE")
     if is_mem:
-        if away is not None:
-            xr, xp, _ = topo.addr(away)
-            g.wait_ge(S.ld, 16)
-            g.remote_dma(T.ql[:, ocol:ocol + 32], T.qd[:, :], S["qa%d" % oi], S.sent, xp, xr, _pick(eng, NQ))
-            sent += NQ
+        n_c = {"ident": 0, "ee": 0}
+        for h in jobs:
+            if core in jobs[h][1]:
+                n_c[jobs[h][0]] += _split(_y_engines(h, blocks, topo), len(jobs[h][1]))[0]
+        n_ident, n_ee = n_c["ident"], n_c["ee"]
         kd, per, sets = _kv_split(core, servers, topo)
         for lsem, asem, c0 in ((S.kld, S.ka, o), (S.vld, S.va, o + 128)):
             trs = []
@@ -263,102 +190,100 @@ def _server(g, core, T, topo, plan):
                 sent += per
             g.wait_ge(lsem, 16)
             g.remote_dma_fused(trs, local_sem=S.sent)
-        pe.wait_ge(S.kld, 16)
+    else:
+        n_ident = n_ee = 1
+        name, dests = jobs[core]
+        buf, sem = (T.ident, S.sB) if name == "ident" else (T.ee, S.sEE)
+        w, sets = _split(eng, len(dests))
+        trs = []
+        for x, es in zip(dests, sets):
+            xr, xp, _ = topo.addr(x)
+            trs.append(RemoteDMATransfer(dst_ids=[DstId(rid=xr, pnc=xp)], dma_engine_mask=_pick(es, w),
+                                         remote_sem=sem, src=buf[:, :], dst=buf[:, :]))
+            sent += w
+        g.wait_ge(S.sA0, 2)
+        steps = ["ident", "send", "rr"] if name == "ident" else ["rr", "ident", "send"]
+        for st in steps:
+            if st == "ident":
+                g.affine_select(T.ident[:, :], T.zero[:, :], [[-1, 128]], AluOpType.not_equal, 1.0, 0, 1) \
+                    .then_inc(S.sB, 1)
+            elif st == "rr":
+                g.affine_select(T.rr[0:32, :], T.zero[0:32, :], [[0, 4], [-1, 32]], AluOpType.not_equal, 1.0, 0, 1) \
+                    .then_inc(S.sRr, 1)
+            else:
+                g.wait_ge(sem, 1)
+                g.remote_dma_fused(trs, local_sem=S.sent)
+        pe.wait_ge(S.sRr, 1)
+        pe.matmul(T.ep[:, 0:128], T.rr[0:32, :], T.rr[0:32, :], True, True).then_inc(S.sEp, 1)
+        dve.wait_ge(S.sEp, 1)
+        dve.tensor_copy(T.ee[:, :], T.ep[:, 0:128]).then_inc(S.sEE, 1)
     n_kv = sum(_kv_split(x, servers, topo)[1] for x in mem if x != core)
-    pe.wait_ge(S.ka, n_kv)
 
-    tb = [T.t0, T.t1]
-    col = 0
-    stores = 0
-    for p, blk in enumerate(passes[core]):
-        nb = len(blk)
-        Q = 32 * nb
-        P0 = 256 * p
-        Y0 = 128 * p
-        far = [c for c in blk if c != core]
-        pe.wait_ge(S["qa%d" % p], NQ * len(far) + 16 * (nb - len(far)))
-        for kb in range(2):
-            inc(pe.matmul(T.pa[0:Q, 128 * kb:128 * kb + 128], T.ql[:, col:col + Q],
-                          T.kv[:, 256 * kb:256 * kb + 128], True, True), "sS")
-        dve.wait_ge(S.sS, n["sS"])
-        inc(dve.tensor_reduce(T.nm[0:Q, p:p + 1], T.pa[0:Q, 0:256], AxisListType.X, AluOpType.max, negate=True), "sM")
-        act.wait_ge(S.sM, n["sM"])
-        inc(act.activation(T.pp[0:Q, P0:P0 + 256], T.pa[0:Q, 0:256], ActivationFunctionType.Exp,
-                           bias=T.nm[0:Q, p:p + 1], scale=1.0, accum_out=T.ls[0:Q, p:p + 1]), "sE")
-        pe.wait_ge(S.sE, n["sE"])
-        if p == 0:
-            pe.wait_ge(S.sB, n_ident)
-        for kb in range(2):
-            inc(pe.matmul(tb[kb][:, 0:Q], T.pp[0:Q, P0 + 128 * kb:P0 + 128 * kb + 128],
-                          T.ident[0:Q, 0:Q], True, True), "sT%d" % kb)
-        for kb in range(2):
-            act.wait_ge(S["sT%d" % kb], n["sT%d" % kb])
-            inc(act.activation(T.pt[:, P0 + Q * kb:P0 + Q * kb + Q], tb[kb][:, 0:Q], ActivationFunctionType.Copy),
-                "sC%d" % kb)
-        dve.wait_ge(S.sE, n["sE"])
-        inc(dve.reciprocal(T.rs[0:Q, p:p + 1], T.ls[0:Q, p:p + 1]), "sR1")
-        dve.wait_ge(S.sR1, n["sR1"])
-        if p == 0:
-            dve.wait_ge(S.sA, 4)
-        inc(dve.tensor_scalar(T.mr[0:Q, 8 * p:8 * p + nb], T.mk[0:Q, 0:nb], T.rs[0:Q, p:p + 1], None,
-                              AluOpType.mult), "sR2")
-        if p == 0:
-            pe.wait_ge(S.sEE, 1)
-        if n.get("sO", 0):
-            pe.wait_ge(S.sO, n["sO"])
-        pe.wait_ge(S.sR2, n["sR2"])
-        inc(pe.matmul(T.pr[:, 0:nb], T.ee[0:Q, :], T.mr[0:Q, 8 * p:8 * p + nb], True, True), "sRR")
-        if p == 0:
-            if is_mem:
-                pe.wait_ge(S.vld, 16)
-            pe.wait_ge(S.va, n_kv)
-        pe.wait_ge(S.sC0, n["sC0"])
-        pe.wait_ge(S.sC1, n["sC1"])
-        for b in range(nb):
-            for fb in range(4):
-                for kb in range(2):
-                    inc(pe.matmul(T.yt[32 * fb:32 * fb + 32, 32 * b:32 * b + 32],
-                                  T.pt[:, P0 + Q * kb + 32 * b:P0 + Q * kb + 32 * b + 32],
-                                  T.kv[:, 256 * kb + 128 + 32 * fb:256 * kb + 128 + 32 * fb + 32],
-                                  kb == 0, kb == 1), "sY")
-        dve.wait_ge(S.sRR, n["sRR"])
-        dve.wait_ge(S.sY, n["sY"])
-        for b in range(nb):
-            inc(dve.tensor_scalar(T.ys[:, Y0 + 32 * b:Y0 + 32 * b + 32], T.yt[:, 32 * b:32 * b + 32],
-                                  T.pr[:, b:b + 1], None, AluOpType.mult), "sO")
-        if far:
-            g.wait_ge(S.sO, n["sO"])
-            trs = []
-            for b, c in enumerate(blk):
-                if c == core:
-                    continue
-                w = place[c][2]
-                m = 0
-                for e in eng[len(trs) * w:(len(trs) + 1) * w]:
-                    m |= 1 << e
-                cr, cp, _ = topo.addr(c)
-                trs.append(RemoteDMATransfer(dst_ids=[DstId(rid=cr, pnc=cp)], dma_engine_mask=m, remote_sem=S.yarr,
-                                             src=T.ys[:, Y0 + 32 * b:Y0 + 32 * b + 32], dst=T.yl[:, :]))
-                sent += w
-            g.remote_dma_fused(trs, local_sem=S.sent)
-        if core in blk:
-            b = blk.index(core)
-            _store_y([g.sync], T, T.ys[:, Y0 + 32 * b:Y0 + 32 * b + 32], S.sO, n["sO"])
-            stores += 64
-        col += Q
-    if away is not None:
-        _store_y([g.sync], T, T.yl, S.yarr, ow)
-        stores += 64
+    if is_mem:
+        pe.wait_ge(S.kld, 16)
+    pe.wait_ge(S.ka, n_kv)
+    pe.wait_ge(S.qa, NQ * nfar + 16 * (nb - nfar))
+    for kb in range(2):
+        pe.matmul(T.pa[0:Q, 128 * kb:128 * kb + 128], T.ql[:, 0:Q], T.kv[:, 256 * kb:256 * kb + 128], True, True) \
+            .then_inc(S.sS, 1)
+    pe.wait_ge(S.sE, 1)
+    pe.wait_ge(S.sB, n_ident)
+    for kb in range(2):
+        pe.matmul(TB[kb][:, 0:Q], T.pp[0:Q, 128 * kb:128 * kb + 128], T.ident[0:Q, 0:Q], True, True) \
+            .then_inc(S["sT" + "ab"[kb]], 1)
+    if is_mem:
+        pe.wait_ge(S.vld, 16)
+    pe.wait_ge(S.va, n_kv)
+    pe.wait_ge(S.sC, 2)
+    for b in range(nb):
+        for fb in range(4):
+            for kb in range(2):
+                pe.matmul(Z[b][32 * fb:32 * fb + 32, 0:32], T.pt[:, Q * kb + 32 * b:Q * kb + 32 * b + 32],
+                          T.kv[:, 256 * kb + 128 + 32 * fb:256 * kb + 128 + 32 * fb + 32],
+                          kb == 0, kb == 1).then_inc(S["sY%d" % b], 1)
+        if b == 0:
+            pe.wait_ge(S.sEE, n_ee)
+            pe.wait_ge(S.sRb, 1)
+            pe.matmul(Z[0][:, 64:64 + nb], T.ee[0:Q, :], T.mr[0:Q, 0:nb], True, True).then_inc(S.sP, 1)
+
+    dve.wait_ge(S.sS, 2)
+    dve.tensor_reduce(T.nm[0:Q, 0:1], T.pa[0:Q, 0:256], AxisListType.X, AluOpType.max, negate=True).then_inc(S.sM, 1)
+    dve.wait_ge(S.sE, 1)
+    dve.reciprocal(T.rs[0:Q, 0:1], T.ls[0:Q, 0:1]).then_inc(S.sRa, 1)
+    dve.wait_ge(S.sRa, 1)
+    dve.wait_ge(S.sA, 4)
+    dve.tensor_scalar(T.mr[0:Q, 0:nb], T.mk[0:Q, 0:nb], T.rs[0:Q, 0:1], None, MUL).then_inc(S.sRb, 1)
+    dve.wait_ge(S.sP, 1)
+    for b in range(nb):
+        dve.wait_ge(S["sY%d" % b], 8)
+        dve.tensor_scalar(T.ys[:, 32 * b:32 * b + 32], Z[b][:, 0:32], Z[0][:, 64 + b:64 + b + 1], None, MUL) \
+            .then_inc(S["sO%d" % b], 1)
+
+    act.wait_ge(S.sM, 1)
+    act.activation(T.pp[0:Q, 0:256], T.pa[0:Q, 0:256], EXP, bias=T.nm[0:Q, 0:1], scale=1.0,
+                   accum_out=T.ls[0:Q, 0:1]).then_inc(S.sE, 1)
+    for kb in range(2):
+        act.wait_ge(S["sT" + "ab"[kb]], 1)
+        act.activation(T.pt[:, Q * kb:Q * kb + Q], TB[kb][:, 0:Q], COPY).then_inc(S.sC, 1)
+
+    for b, c in enumerate(blk):
+        if c == core:
+            _store_y([g.sync, act], T, T.ys[:, 32 * b:32 * b + 32], S["sO%d" % b], 1)
+        else:
+            cr, cp, _ = topo.addr(c)
+            g.wait_ge(S["sO%d" % b], 1)
+            g.remote_dma(T.yl[:, :], T.ys[:, 32 * b:32 * b + 32], S.yarr, S.sent, cp, cr, _pick(eng, len(eng)))
+            sent += len(eng)
     g.wait_ge(S.sent, sent)
-    if stores:
-        g.wait_ge(S.st, stores)
+    if is_mem:
+        g.wait_ge(S.st, 64)
 
 
 def rank_program(g, core, T, topo):
     plan = _plan(T, topo)
-    if T.rank_of(core) is None and core not in plan[1]:
+    if T.rank_of(core) is None and core not in plan[2]:
         return
-    if core in plan[1]:
+    if core in plan[2]:
         _server(g, core, T, topo, plan)
     else:
         _client(g, core, T, topo, plan)

from concourse.bass import DstId, RemoteDMATransfer
from concourse.mybir import AluOpType, AxisListType, ActivationFunctionType

NQ = 8
NR = 2
BF, F32 = "bfloat16", "float32"

SCRATCH = {
    "qd": ("dram", [128, 32], BF),
    "qr": ("dram", [2, 128, 32], BF),
    "yl": ("sbuf", [128, 32], BF),
    "kv": ("sbuf", [128, 512], BF),
    "ql": ("sbuf", [128, 128], BF),
    "zero": ("sbuf", [128, 128], BF),
    "ident": ("sbuf", [128, 128], BF),
    "rr": ("sbuf", [128, 128], BF),
    "ee": ("sbuf", [128, 128], BF),
    "mk": ("sbuf", [128, 8], BF),
    "mr": ("sbuf", [128, 8], BF),
    "nm": ("sbuf", [128, 4], F32),
    "ls": ("sbuf", [128, 4], F32),
    "rs": ("sbuf", [128, 4], F32),
    "pp": ("sbuf", [128, 256], BF),
    "pt": ("sbuf", [128, 256], BF),
    "ys": ("sbuf", [128, 96], BF),
    "pa": ("psum", [128, 512], F32),
    "t0": ("psum", [128, 512], F32),
    "t1": ("psum", [128, 512], F32),
    "z0": ("psum", [128, 512], F32),
    "z1": ("psum", [128, 512], F32),
    "z2": ("psum", [128, 512], F32),
    "ep": ("psum", [128, 512], F32),
}
SEMAPHORES = ["ld", "rel0", "rel1", "sent", "yarr", "st", "kld", "vld", "ka", "va", "qa",
              "sA0", "sA", "sB", "sRr", "sEp", "sEE", "sS", "sM", "sE", "sTa", "sTb", "sC", "sRa", "sRb", "sP",
              "sY0", "sY1", "sY2", "sO0", "sO1", "sO2"]


def _bits(mask):
    return [i for i in range(16) if (mask >> i) & 1]


def _pick(bits, n):
    step = len(bits) // n
    m = 0
    for b in bits[::step][:n]:
        m |= 1 << b
    return m


def _split(bits, k):
    per = 1
    while per * 2 * k <= len(bits):
        per *= 2
    return per, [bits[i * per:(i + 1) * per] for i in range(k)]


def _plan(T, topo):
    cores = list(T.cores)
    mem = [cores[j] for j in T.tables["MEM"]]
    clients = [c for c in cores if c not in mem]
    home = topo.chip(mem[0])
    easy = [c for c in clients if all(topo.may_write(s, c) for s in mem)]
    hard = [c for c in clients if c not in easy]
    ports = [h for h in range(max(cores) + 1) if topo.chip(h) == home and (h in mem or T.rank_of(h) is None)
             and all(topo.may_write(h, c) for c in hard)]
    pmem = [s for s in ports if s in mem]
    helpers = sorted([h for h in ports if h not in mem], key=lambda h: topo.die(h) == topo.die(pmem[0]))
    early = [c for c in hard if topo.may_write(c, ports[0])]
    late = [c for c in hard if c not in early]
    via = {c: None for c in clients}
    for c in late:
        via[c] = [x for x in early if topo.chip(x) == topo.chip(c)][0]
    servers = mem + helpers
    blocks = {s: [] for s in servers}
    groups = [late[i:i + 2] for i in range(0, len(late), 2)] + [early[i:i + 2] for i in range(0, len(early), 2)]
    for h, grp in zip(pmem[:1] + helpers, groups):
        blocks[h] = list(grp)
    plain = [s for s in mem if not blocks[s]] or mem
    blocks[plain[0]] = blocks[plain[0]] + easy
    for s in mem:
        blocks[s] = blocks[s] + [s]
    server = {c: s for s in servers for c in blocks[s]}
    return mem, helpers, servers, server, via, blocks


def _kv_split(s, servers, topo):
    kd = [x for x in servers if x != s]
    both = topo.mask(s, kd[0])
    for x in kd:
        both &= topo.mask(s, x)
    per, sets = _split(_bits(both), len(kd))
    return kd, per, sets


def _y_engines(s, blocks, topo):
    dsts = [c for c in blocks[s] if c != s]
    common = topo.mask(s, dsts[0])
    for d in dsts:
        common &= topo.mask(s, d)
    return _bits(common)


def _jobs(mem, helpers):
    return dict(zip(helpers, [("ident", list(mem))] + [("ee", [m]) for m in mem]))


def _store_y(queues, T, src, sem_wait, val):
    for q in queues:
        q.wait_ge(sem_wait, val)
    for fb in range(4):
        q = queues[fb % len(queues)]
        q.dma_start(T.y[:, 32 * fb:32 * fb + 32], src[32 * fb:32 * fb + 32, :]).then_inc(T.sem.st, 16)


def _client(g, core, T, topo, plan):
    mem, helpers, servers, server, via, blocks = plan
    g.sync.dma_start(T.qd[:, :], T.q[:, :]).then_inc(T.sem.ld, 16)
    g.wait_ge(T.sem.ld, 16)
    sent = 0

    def to_server(c, src):
        s = server[c]
        rid, pid, _ = topo.addr(s)
        col = 32 * blocks[s].index(c)
        g.remote_dma(T.ql[:, col:col + 32], src, T.sem.qa, T.sem.sent, pid, rid,
                     _pick(_bits(topo.mask(core, s)), NQ))

    if via[core] is None:
        to_server(core, T.qd[:, :])
        sent += NQ
        for k, c in enumerate([c for c in via if via[c] == core]):
            g.wait_ge(T.sem["rel%d" % k], NR)
            to_server(c, T.qr[k])
            sent += NQ
    else:
        x = via[core]
        k = [c for c in via if via[c] == x].index(core)
        xr, xp, _ = topo.addr(x)
        g.remote_dma(T.qr[k], T.qd[:, :], T.sem["rel%d" % k], T.sem.sent, xp, xr,
                     _pick(_bits(topo.mask(core, x)), NR))
        sent += NR
    _store_y([g.sync, g.scalar], T, T.yl, T.sem.yarr, len(_y_engines(server[core], blocks, topo)))
    g.wait_ge(T.sem.sent, sent)
    g.wait_ge(T.sem.st, 64)


def _server(g, core, T, topo, plan):
    mem, helpers, servers, server, via, blocks = plan
    S = T.sem
    pe, dve, act = g.tensor, g.vector, g.scalar
    is_mem = core in mem
    blk = blocks[core]
    nb = len(blk)
    Q = 32 * nb
    nfar = len([c for c in blk if c != core])
    EXP, COPY = ActivationFunctionType.Exp, ActivationFunctionType.Copy
    MUL = AluOpType.mult
    TB, Z = [T.t0, T.t1], [T.z0, T.z1, T.z2]

    if is_mem:
        o = 256 * mem.index(core)
        ocol = 32 * blk.index(core)
        g.sync.dma_start(T.kv[:, o:o + 128], T.k[:, :]).then_inc(S.kld, 16)
        act.dma_start(T.kv[:, o + 128:o + 256], T.v[:, :]).then_inc(S.vld, 16)
        g.sync.dma_start(T.ql[:, ocol:ocol + 32], T.q[:, :]).then_inc(S.qa, 16)

    dve.memset(T.zero[:, :], 0.0).then_inc(S.sA0, 1)
    dve.memset(T.mk[:, :], 0.0).then_inc(S.sA0, 1)
    act.wait_ge(S.sA0, 2)
    for b in range(4):
        act.activation(T.mk[32 * b:32 * b + 32, b:b + 1], T.zero[32 * b:32 * b + 32, 0:1], EXP).then_inc(S.sA, 1)

    eng = _y_engines(core, blocks, topo)
    jobs = _jobs(mem, helpers)
    sent = 0
    if is_mem:
        n_c = {"ident": 0, "ee": 0}
        for h in jobs:
            if core in jobs[h][1]:
                n_c[jobs[h][0]] += _split(_y_engines(h, blocks, topo), len(jobs[h][1]))[0]
        n_ident, n_ee = n_c["ident"], n_c["ee"]
        kd, per, sets = _kv_split(core, servers, topo)
        for lsem, asem, c0 in ((S.kld, S.ka, o), (S.vld, S.va, o + 128)):
            trs = []
            for x, es in zip(kd, sets):
                xr, xp, _ = topo.addr(x)
                trs.append(RemoteDMATransfer(dst_ids=[DstId(rid=xr, pnc=xp)], dma_engine_mask=_pick(es, per),
                                             remote_sem=asem, src=T.kv[:, c0:c0 + 128], dst=T.kv[:, c0:c0 + 128]))
                sent += per
            g.wait_ge(lsem, 16)
            g.remote_dma_fused(trs, local_sem=S.sent)
    else:
        n_ident = n_ee = 1
        name, dests = jobs[core]
        buf, sem = (T.ident, S.sB) if name == "ident" else (T.ee, S.sEE)
        w, sets = _split(eng, len(dests))
        trs = []
        for x, es in zip(dests, sets):
            xr, xp, _ = topo.addr(x)
            trs.append(RemoteDMATransfer(dst_ids=[DstId(rid=xr, pnc=xp)], dma_engine_mask=_pick(es, w),
                                         remote_sem=sem, src=buf[:, :], dst=buf[:, :]))
            sent += w
        g.wait_ge(S.sA0, 2)
        steps = ["ident", "send", "rr"] if name == "ident" else ["rr", "ident", "send"]
        for st in steps:
            if st == "ident":
                g.affine_select(T.ident[:, :], T.zero[:, :], [[-1, 128]], AluOpType.not_equal, 1.0, 0, 1) \
                    .then_inc(S.sB, 1)
            elif st == "rr":
                g.affine_select(T.rr[0:32, :], T.zero[0:32, :], [[0, 4], [-1, 32]], AluOpType.not_equal, 1.0, 0, 1) \
                    .then_inc(S.sRr, 1)
            else:
                g.wait_ge(sem, 1)
                g.remote_dma_fused(trs, local_sem=S.sent)
        pe.wait_ge(S.sRr, 1)
        pe.matmul(T.ep[:, 0:128], T.rr[0:32, :], T.rr[0:32, :], True, True).then_inc(S.sEp, 1)
        dve.wait_ge(S.sEp, 1)
        dve.tensor_copy(T.ee[:, :], T.ep[:, 0:128]).then_inc(S.sEE, 1)
    n_kv = sum(_kv_split(x, servers, topo)[1] for x in mem if x != core)

    if is_mem:
        pe.wait_ge(S.kld, 16)
    pe.wait_ge(S.ka, n_kv)
    pe.wait_ge(S.qa, NQ * nfar + 16 * (nb - nfar))
    for kb in range(2):
        pe.matmul(T.pa[0:Q, 128 * kb:128 * kb + 128], T.ql[:, 0:Q], T.kv[:, 256 * kb:256 * kb + 128], True, True) \
            .then_inc(S.sS, 1)
    pe.wait_ge(S.sE, 1)
    pe.wait_ge(S.sB, n_ident)
    for kb in range(2):
        pe.matmul(TB[kb][:, 0:Q], T.pp[0:Q, 128 * kb:128 * kb + 128], T.ident[0:Q, 0:Q], True, True) \
            .then_inc(S["sT" + "ab"[kb]], 1)
    if is_mem:
        pe.wait_ge(S.vld, 16)
    pe.wait_ge(S.va, n_kv)
    pe.wait_ge(S.sC, 2)
    for b in range(nb):
        for fb in range(4):
            for kb in range(2):
                pe.matmul(Z[b][32 * fb:32 * fb + 32, 0:32], T.pt[:, Q * kb + 32 * b:Q * kb + 32 * b + 32],
                          T.kv[:, 256 * kb + 128 + 32 * fb:256 * kb + 128 + 32 * fb + 32],
                          kb == 0, kb == 1).then_inc(S["sY%d" % b], 1)
        if b == 0:
            pe.wait_ge(S.sEE, n_ee)
            pe.wait_ge(S.sRb, 1)
            pe.matmul(Z[0][:, 64:64 + nb], T.ee[0:Q, :], T.mr[0:Q, 0:nb], True, True).then_inc(S.sP, 1)

    dve.wait_ge(S.sS, 2)
    dve.tensor_reduce(T.nm[0:Q, 0:1], T.pa[0:Q, 0:256], AxisListType.X, AluOpType.max, negate=True).then_inc(S.sM, 1)
    dve.wait_ge(S.sE, 1)
    dve.reciprocal(T.rs[0:Q, 0:1], T.ls[0:Q, 0:1]).then_inc(S.sRa, 1)
    dve.wait_ge(S.sRa, 1)
    dve.wait_ge(S.sA, 4)
    dve.tensor_scalar(T.mr[0:Q, 0:nb], T.mk[0:Q, 0:nb], T.rs[0:Q, 0:1], None, MUL).then_inc(S.sRb, 1)
    dve.wait_ge(S.sP, 1)
    for b in range(nb):
        dve.wait_ge(S["sY%d" % b], 8)
        dve.tensor_scalar(T.ys[:, 32 * b:32 * b + 32], Z[b][:, 0:32], Z[0][:, 64 + b:64 + b + 1], None, MUL) \
            .then_inc(S["sO%d" % b], 1)

    act.wait_ge(S.sM, 1)
    act.activation(T.pp[0:Q, 0:256], T.pa[0:Q, 0:256], EXP, bias=T.nm[0:Q, 0:1], scale=1.0,
                   accum_out=T.ls[0:Q, 0:1]).then_inc(S.sE, 1)
    for kb in range(2):
        act.wait_ge(S["sT" + "ab"[kb]], 1)
        act.activation(T.pt[:, Q * kb:Q * kb + Q], TB[kb][:, 0:Q], COPY).then_inc(S.sC, 1)

    for b, c in enumerate(blk):
        if c == core:
            _store_y([g.sync, act], T, T.ys[:, 32 * b:32 * b + 32], S["sO%d" % b], 1)
        else:
            cr, cp, _ = topo.addr(c)
            g.wait_ge(S["sO%d" % b], 1)
            g.remote_dma(T.yl[:, :], T.ys[:, 32 * b:32 * b + 32], S.yarr, S.sent, cp, cr, _pick(eng, len(eng)))
            sent += len(eng)
    g.wait_ge(S.sent, sent)
    if is_mem:
        g.wait_ge(S.st, 64)


def rank_program(g, core, T, topo):
    plan = _plan(T, topo)
    if T.rank_of(core) is None and core not in plan[2]:
        return
    if core in plan[2]:
        _server(g, core, T, topo, plan)
    else:
        _client(g, core, T, topo, plan)
